import numpy as np
import ml_dtypes


def mxq(x, axis, fmt="e4m3"):
    dtype, down = {"e4m3": (ml_dtypes.float8_e4m3fn, 7), "e5m2": (ml_dtypes.float8_e5m2, 14)}[fmt]
    v = np.moveaxis(np.asarray(x, np.float32).astype(ml_dtypes.bfloat16).astype(np.float64), axis, -1)
    blocks = v.reshape(v.shape[:-1] + (-1, 32))
    amax = np.abs(blocks).max(-1, keepdims=True)
    byte = np.maximum(np.where(amax > 0, np.frexp(amax)[1] - 1 + 127, 0) - down, 1)
    scale = np.exp2(byte - 127.0)
    codes = (blocks / scale).astype(np.float32).astype(dtype).astype(np.float64)
    return np.moveaxis((codes * scale).reshape(v.shape), -1, axis)


WIDE = False


def mx_kscale(k):
    if not WIDE:
        return np.ones(k)
    levels = np.array([10, -10, 5, -5, 0])
    if k % 512:
        return np.exp2(np.random.permutation(np.resize(levels, k // 32))).repeat(32)
    a = np.empty((k // 512, 16))
    for p in range(k // 512):
        a[p, :8] = np.random.permutation(np.resize(levels, 8))
        for g in range(8):
            far = levels[np.abs(levels - a[p, g]) >= 10]
            a[p, g + 8] = far[np.random.randint(len(far))]
    return np.exp2(a.ravel()).repeat(32)


def f64(x):
    return np.asarray(x).astype(np.float64)


def striped(idx):
    return np.tile(idx.reshape(-1, 16).T, (8, 1)).astype(np.uint16)


def unstriped(offs):
    return offs[:16].T.reshape(-1).astype(np.int64)


def striped8(idx):
    return np.concatenate([x.reshape(-1, 16).T for x in idx]).astype(np.uint16)


def runs(offs, k):
    lists = np.stack([offs[16 * r : 16 * r + 16].T.reshape(-1) for r in range(8)]).astype(np.int64)
    return lists[np.arange(k) % 512 // 64]


def pack_weight(w):
    k, n = w.shape
    w = f64(np.asarray(w, np.float32).astype(ml_dtypes.bfloat16)).reshape(k // 32, 32, n)
    amax = np.abs(w).max(1)
    byte = np.clip(np.where(amax > 0, np.frexp(amax)[1] - 1 + 127 - 7, 1), 1, 254)
    scaled = (w * np.exp2(127.0 - byte)[:, None, :]).reshape(k, n).astype(np.float32)
    words = np.ascontiguousarray(scaled.reshape(k // 512, 128, 4, n).transpose(0, 1, 3, 2)).astype(ml_dtypes.float8_e4m3fn).view(np.uint8)
    return words, np.ascontiguousarray(byte.astype(np.uint8).reshape(k // 512, 16, n))


def unpack_weight(words, scales):
    g, p, n, _ = words.shape
    vals = np.ascontiguousarray(words).view(ml_dtypes.float8_e4m3fn).astype(np.float64) * np.repeat(np.exp2(scales.astype(np.float64) - 127.0), 8, axis=1)[..., None]
    return vals.transpose(0, 1, 3, 2).reshape(g * 512, n)


K, T, S, G, H, W, U = 512, 1024, 256, 2048, 512, 128, 512


def setup_inputs():
    n = np.random.standard_normal
    s = mx_kscale(K)[:, None]
    packed_xT = pack_weight(n((K, T)) * s)
    packed_dT = pack_weight(n((K, G)) / s)
    perm = np.random.permutation(S)
    perm2 = np.random.permutation(U)
    return {
        "x_words": packed_xT[0],
        "x_scales": packed_xT[1],
        "d_words": packed_dT[0],
        "d_scales": packed_dT[1],
        "gs": (np.random.uniform(0.5, 1.5, (K, 1)) * s).astype(np.float32),
        "offs": striped(np.random.permutation(T)[:S]),
        "ka": striped8(np.random.randint(0, G, (8, H))),
        "kb": striped8(np.random.randint(0, G, (8, H))),
        "n1": striped(perm[:W]),
        "n2": striped(perm[W:]),
        "kc": striped8(np.random.randint(0, G, (8, H))),
        "kd": striped8(np.random.randint(0, G, (8, H))),
        "n3": striped(perm2[:S]),
        "n4": striped(perm2[S:]),
        "n5": striped(np.random.permutation(S)),
        "n6": striped(np.random.permutation(S)),
    }


def reference(x_words, x_scales, d_words, d_scales, gs, offs, ka, kb, n1, n2, kc, kd, n3, n4, n5, n6):
    d_kc = unpack_weight(d_words, d_scales)[np.arange(K)[:, None], runs(kc, K)]
    d_ka = unpack_weight(d_words, d_scales)[np.arange(K)[:, None], runs(ka, K)]
    xq = unpack_weight(x_words, x_scales)[:, unstriped(offs)]
    d_kb = unpack_weight(d_words, d_scales)[np.arange(K)[:, None], runs(kb, K)]
    h = 0.0625 * (d_ka.T @ xq + d_kb.T @ xq)
    pb = h[:, unstriped(n2)]
    pa = h[:, unstriped(n1)]
    rb = pb - (0.5 * pa)
    ra = np.sqrt((pa) ** 2 + (pb) ** 2 + 0.25)
    ua = np.zeros((H, S))
    ua[:, unstriped(n1)] = ra
    ub = ua.copy()
    ub[:, unstriped(n2)] = rb
    z = f64(gs) * ub
    zq = mxq(z, 0, "e4m3")
    d_kd = unpack_weight(d_words, d_scales)[np.arange(K)[:, None], runs(kd, K)]
    h2 = 0.0625 * (d_kc.T @ zq + d_kd.T @ zq)
    st = h2 - h2[:, unstriped(n5)]
    up = np.maximum(st, st[:, unstriped(n6)])
    ph = np.zeros((H, U))
    ph[:, unstriped(n3)] = st
    out = ph.copy()
    out[:, unstriped(n4)] = up
    return out

@@ -1,0 +1,205 @@
+from contextlib import ExitStack
+
+import concourse.mybir as mybir
+
+K, T, S, G, H, W, U = 512, 1024, 256, 2048, 512, 128, 512
+FLOPS = 4 * 2 * K * H * S
+
+F32 = mybir.dt.float32
+BF16 = mybir.dt.bfloat16
+I32 = mybir.dt.int32
+U32 = mybir.dt.uint32
+U16 = mybir.dt.uint16
+U8 = mybir.dt.uint8
+FP8X4 = mybir.dt.float8_e4m3fn_x4
+ALU = mybir.AluOpType
+ACT = mybir.ActivationFunctionType
+
+P = 128
+PACK = 4
+TILES = H // P
+BLOCKS = K // 32
+SPARE = 16
+HALF = H // 2
+
+
+def tile_picked_atzapolarpagew_none_p_kernel(
+    tc, x_words, x_scales, d_words, d_scales, gs, offs, ka, kb, n1, n2, kc, kd, n3, n4, n5, n6, out
+):
+    nc = tc.nc
+    with ExitStack() as ctx:
+        lists = ctx.enter_context(tc.tile_pool(name="lists", bufs=1))
+        sb = ctx.enter_context(tc.tile_pool(name="sb", bufs=1))
+        psum = ctx.enter_context(tc.psum_pool(name="psum", bufs=1))
+
+        def load_list(src, name):
+            tile = lists.tile(list(src.shape), U16, name=name)
+            nc.sync.dma_start(tile[:], src)
+            return tile
+
+        def load_scale_rows(src, width, name):
+            tile = sb.tile([P, width], U8, name=name, align_bytes=64)
+            rows = src[0].bitcast(I32).unsqueeze(1).broadcast_to([BLOCKS, P // BLOCKS, width // 4])
+            nc.sync.dma_start(tile[:].bitcast(I32), rows)
+            return tile
+
+        def load_words(src, width, name):
+            tile = sb.tile([P, width], I32, name=name, align_bytes=64)
+            nc.sync.dma_start(tile[:], src[0].rearrange("p n t -> p (n t)").bitcast(I32))
+            return tile
+
+        def place_scale_rows(queue, plane, gathered):
+            for r in range(4):
+                queue.dma_start(plane[:].bitcast(I32)[r:P:32, :], gathered[:].bitcast(I32)[8 * r : P : 32, :])
+
+        offs_sb = load_list(offs, "offs_sb")
+        x_scale_table = load_scale_rows(x_scales, T, "x_scale_table")
+        ka_sb = load_list(ka, "ka_sb")
+        d_scale_table = load_scale_rows(d_scales, G, "d_scale_table")
+        kb_sb = load_list(kb, "kb_sb")
+        d_word_table = load_words(d_words, G, "d_word_table")
+        x_word_table = load_words(x_words, T, "x_word_table")
+        n1_sb = load_list(n1, "n1_sb")
+        n2_sb = load_list(n2, "n2_sb")
+        kc_sb = load_list(kc, "kc_sb")
+        kd_sb = load_list(kd, "kd_sb")
+        n5_sb = load_list(n5, "n5_sb")
+        n6_sb = load_list(n6, "n6_sb")
+        n3_sb = load_list(n3, "n3_sb")
+        n4_sb = load_list(n4, "n4_sb")
+        gs_sb = sb.tile([P, PACK], F32, name="gs_sb")
+        nc.sync.dma_start(gs_sb[:], gs.rearrange("(p t) o -> p (t o)", t=PACK))
+
+        plane1 = sb.tile([P, S + 2 * H], U8, name="plane1", align_bytes=64)
+        plane2 = sb.tile([P, 2 * H], U8, name="plane2", align_bytes=64)
+        nc.vector.memset(plane1[:].bitcast(I32), 0)
+        nc.vector.memset(plane2[:].bitcast(I32), 0)
+        h2 = [sb.tile([P, S + SPARE], F32, name=f"h2_{t}") for t in range(TILES)]
+        st = [sb.tile([P, S + SPARE], F32, name=f"st_{t}") for t in range(TILES)]
+        for window in h2 + st:
+            nc.vector.memset(window[:, S:], 0.0)
+
+        bytes1 = sb.tile([P, S + 2 * H], U8, name="bytes1", align_bytes=64)
+        nc.vector.tensor_copy(bytes1[:, :S], x_scale_table[:].indirect(offs_sb[:]))
+        nc.vector.tensor_copy(bytes1[:, S : S + H], d_scale_table[:].indirect(ka_sb[:]))
+        nc.vector.tensor_copy(bytes1[:, S + H :], d_scale_table[:].indirect(kb_sb[:]))
+        place_scale_rows(nc.scalar, plane1, bytes1)
+
+        words1 = sb.tile([P, 2 * H], U32, name="words1", align_bytes=64)
+        x_codes = sb.tile([P, S], U32, name="x_codes", align_bytes=64)
+        nc.vector.tensor_copy(words1[:, :H], d_word_table[:].bitcast(U32).indirect(ka_sb[:]))
+        nc.vector.tensor_copy(words1[:, H:], d_word_table[:].bitcast(U32).indirect(kb_sb[:]))
+        nc.vector.tensor_copy(x_codes[:], x_word_table[:].bitcast(U32).indirect(offs_sb[:]))
+
+        words_by_t = words1[:].rearrange("p (l m t) -> p t l m", l=2, t=PACK)
+        bytes_by_t = plane1[:, S:].rearrange("p (l m t) -> p t l m", l=2, t=PACK)
+        h = []
+        for t in range(TILES):
+            dealt_words = sb.tile([P, 2, P], U32, name=f"dealt_words_{t}", tag="dealt_words", bufs=2, align_bytes=64)
+            dealt_bytes = sb.tile([P, 2, P], U8, name=f"dealt_bytes_{t}", align_bytes=64)
+            nc.vector.tensor_copy(dealt_words[:], words_by_t[:, t])
+            nc.vector.tensor_copy(dealt_bytes[:], bytes_by_t[:, t])
+            acc = psum.tile([P, S], F32, name=f"acc1_{t}")
+            for l in range(2):
+                nc.tensor.matmul_mx(
+                    out=acc[:],
+                    lhsT=dealt_words[:, l, :].bitcast(FP8X4),
+                    lhsT_scale=dealt_bytes[:, l, :],
+                    rhs=x_codes[:].bitcast(FP8X4),
+                    rhs_scale=plane1[:, :S],
+                    start=(l == 0),
+                    stop=(l == 1),
+                )
+            h_t = sb.tile([P, S], F32, name=f"h_{t}")
+            if t == 0:
+                nc.scalar.activation(h_t[:], acc[:], ACT.Copy, scale=0.0625)
+            else:
+                nc.vector.tensor_scalar(h_t[:], acc[:], 0.0625, None, ALU.mult)
+            h.append(h_t)
+
+        squares = sb.tile([P, TILES, W], F32, name="squares")
+        rb = []
+        for t in range(TILES):
+            pair = sb.tile([P, 2, W], F32, name=f"pair_{t}", tag=f"pair_{t}", align_bytes=64)
+            nc.scalar.activation(pair[:, 0, :], h[t][:].indirect(n1_sb[:]), ACT.Copy)
+            nc.scalar.activation(pair[:, 1, :], h[t][:].indirect(n2_sb[:]), ACT.Copy)
+            rb_t = sb.tile([P, W], F32, name=f"rb_{t}")
+            nc.vector.scalar_tensor_tensor(rb_t[:], pair[:, 0, :], -0.5, pair[:, 1, :], ALU.mult, ALU.add)
+            rb.append(rb_t)
+            sq = sb.tile([P, 2, W], F32, name=f"sq_{t}", tag=f"sq_{t}", align_bytes=64)
+            nc.vector.tensor_tensor(sq[:], pair[:], pair[:], ALU.mult)
+            nc.vector.scalar_tensor_tensor(squares[:, t, :], sq[:, 0, :], 0.25, sq[:, 1, :], ALU.add, ALU.add)
+
+        bytes2 = sb.tile([P, 2 * H], U8, name="bytes2", tag=f"pair_{TILES - 1}", align_bytes=64)
+        nc.vector.tensor_copy(bytes2[:, :H], d_scale_table[:].indirect(kc_sb[:]))
+        nc.vector.tensor_copy(bytes2[:, H:], d_scale_table[:].indirect(kd_sb[:]))
+        place_scale_rows(nc.sync, plane2, bytes2)
+
+        def gather_half_of_codes(half, tag):
+            codes = sb.tile([P, 2, HALF], U32, name=f"codes2_{half}", tag=tag, align_bytes=64)
+            columns = slice(half * HALF // 16, (half + 1) * HALF // 16)
+            for l, picks in enumerate((kc_sb, kd_sb)):
+                nc.vector.tensor_copy(codes[:, l, :], d_word_table[:].bitcast(U32).indirect(picks[:, columns]))
+            return codes
+
+        codes2 = [gather_half_of_codes(0, f"sq_{TILES - 1}")]
+
+        ub = [sb.tile([P, S], F32, name=f"ub_{t}") for t in range(TILES)]
+        for t in range(TILES):
+            nc.scalar.activation(ub[t][:].indirect(n2_sb[:]), rb[t][:], ACT.Copy)
+        ra = sb.tile([P, TILES, W], F32, name="ra")
+        nc.scalar.activation(ra[:], squares[:], ACT.Sqrt)
+        token_halves = [slice(0, S // 2), slice(S // 2, S)]
+        z = sb.tile([P, S, PACK], BF16, name="z", tag="z", align_bytes=64)
+        for t in range(TILES):
+            nc.scalar.activation(ub[t][:].indirect(n1_sb[:]), ra[:, t, :], ACT.Copy)
+            pieces = token_halves if t == TILES - 1 else [slice(0, S)]
+            for cols in pieces:
+                nc.vector.tensor_scalar(z[:, cols, t], ub[t][:, cols], gs_sb[:, t : t + 1], None, ALU.mult)
+
+        z_codes = sb.tile([P, S], U32, name="z_codes", align_bytes=64)
+        z_plane = sb.tile([P, S], U8, name="z_plane", align_bytes=64)
+        for cols in token_halves:
+            nc.vector.quantize_mx(
+                out=z_codes[:, cols].bitcast(FP8X4),
+                scales=z_plane[:, cols],
+                in_=z[:, cols, :].rearrange("p n t -> p (n t)"),
+            )
+        codes2.append(gather_half_of_codes(1, "z"))
+
+        for t in range(TILES):
+            acc = psum.tile([P, S], F32, name=f"acc2_{t}")
+            half, first = divmod(t * P, HALF)
+            for cols in token_halves if t == 0 else [slice(0, S)]:
+                for l in range(2):
+                    nc.tensor.matmul_mx(
+                        out=acc[:, cols],
+                        lhsT=codes2[half][:, l, first : first + P].bitcast(FP8X4),
+                        lhsT_scale=plane2[:, l * H + t * P : l * H + (t + 1) * P],
+                        rhs=z_codes[:, cols].bitcast(FP8X4),
+                        rhs_scale=z_plane[:, cols],
+                        start=(l == 0),
+                        stop=(l == 1),
+                    )
+            if t == 0:
+                nc.scalar.activation(h2[t][:, :S], acc[:], ACT.Copy, scale=0.0625)
+            else:
+                nc.vector.tensor_scalar(h2[t][:, :S], acc[:], 0.0625, None, ALU.mult)
+
+        for t in range(TILES):
+            at_n5 = sb.tile([P, S], F32, name=f"at_n5_{t}")
+            nc.scalar.activation(at_n5[:], h2[t][:].indirect(n5_sb[:]), ACT.Copy)
+            nc.vector.tensor_tensor(st[t][:, :S], h2[t][:, :S], at_n5[:], ALU.subtract)
+        up = []
+        for t in range(TILES):
+            at_n6 = sb.tile([P, S], F32, name=f"at_n6_{t}")
+            nc.scalar.activation(at_n6[:], st[t][:].indirect(n6_sb[:]), ACT.Copy)
+            up_t = sb.tile([P, S], F32, name=f"up_{t}")
+            nc.vector.tensor_tensor(up_t[:], st[t][:, :S], at_n6[:], ALU.max)
+            up.append(up_t)
+        page = [sb.tile([P, U], F32, name=f"page_{t}") for t in range(TILES)]
+        for t in range(TILES):
+            nc.scalar.activation(page[t][:].indirect(n3_sb[:]), st[t][:, :S], ACT.Copy)
+        for t in range(TILES):
+            nc.scalar.activation(page[t][:].indirect(n4_sb[:]), up[t][:], ACT.Copy)
+            nc.sync.dma_start(out[t * P : (t + 1) * P, :], page[t][:])

@@ -70,6 +70,11 @@ def tile_picked_atzapolarpagew_none_p_kernel(
         gs_sb = sb.tile([P, PACK], F32, name="gs_sb")
         nc.sync.dma_start(gs_sb[:], gs.rearrange("(p t) o -> p (t o)", t=PACK))
 
+        one = sb.tile([P, 1], F32, name="one")
+        unread = sb.tile([P, 1], F32, name="unread")
+        nc.vector.memset(one[:], 1.0)
+        nc.scalar.activation(unread[:], one[:], ACT.Sqrt)
+
         plane1 = sb.tile([P, S + 2 * H], U8, name="plane1", align_bytes=64)
         plane2 = sb.tile([P, 2 * H], U8, name="plane2", align_bytes=64)
         nc.vector.memset(plane1[:].bitcast(I32), 0)

@@ -48,14 +48,34 @@ def tile_picked_atzapolarpagew_none_p_kernel(
             nc.sync.dma_start(tile[:], src[0].rearrange("p n t -> p (n t)").bitcast(I32))
             return tile
 
-        def place_scale_rows(queue, plane, gathered):
+        def place_scale_rows(queues, plane, gathered):
             for r in range(4):
-                queue.dma_start(plane[:].bitcast(I32)[r:P:32, :], gathered[:].bitcast(I32)[8 * r : P : 32, :])
+                queues[r % len(queues)].dma_start(plane[:].bitcast(I32)[r:P:32, :], gathered[:].bitcast(I32)[8 * r : P : 32, :])
 
-        offs_sb = load_list(offs, "offs_sb")
+        token_halves = [slice(0, S // 2), slice(S // 2, S)]
+
+        def product(t, words, scales, codes, plane, result):
+            for cols in token_halves if t == 0 else [slice(0, S)]:
+                acc = psum.tile([P, cols.stop - cols.start], F32, name="acc", bufs=8)
+                for l in range(2):
+                    nc.tensor.matmul_mx(
+                        out=acc[:],
+                        lhsT=words[:, l, :].bitcast(FP8X4),
+                        lhsT_scale=scales[:, l, :],
+                        rhs=codes[:, cols].bitcast(FP8X4),
+                        rhs_scale=plane[:, cols],
+                        start=(l == 0),
+                        stop=(l == 1),
+                    )
+                if t == 0:
+                    nc.scalar.activation(result[:, cols], acc[:], ACT.Copy, scale=0.0625)
+                else:
+                    nc.vector.tensor_scalar(result[:, cols], acc[:], 0.0625, None, ALU.mult)
+
         x_scale_table = load_scale_rows(x_scales, T, "x_scale_table")
-        ka_sb = load_list(ka, "ka_sb")
+        offs_sb = load_list(offs, "offs_sb")
         d_scale_table = load_scale_rows(d_scales, G, "d_scale_table")
+        ka_sb = load_list(ka, "ka_sb")
         kb_sb = load_list(kb, "kb_sb")
         d_word_table = load_words(d_words, G, "d_word_table")
         x_word_table = load_words(x_words, T, "x_word_table")
@@ -84,11 +104,11 @@ def tile_picked_atzapolarpagew_none_p_kernel(
         for window in h2 + st:
             nc.vector.memset(window[:, S:], 0.0)
 
-        bytes1 = sb.tile([P, S + 2 * H], U8, name="bytes1", align_bytes=64)
+        bytes1 = sb.tile([P, S + 2 * H], U8, name="bytes1", tag="odd", align_bytes=64)
         nc.vector.tensor_copy(bytes1[:, :S], x_scale_table[:].indirect(offs_sb[:]))
         nc.vector.tensor_copy(bytes1[:, S : S + H], d_scale_table[:].indirect(ka_sb[:]))
         nc.vector.tensor_copy(bytes1[:, S + H :], d_scale_table[:].indirect(kb_sb[:]))
-        place_scale_rows(nc.scalar, plane1, bytes1)
+        place_scale_rows((nc.scalar,), plane1, bytes1)
 
         words1 = sb.tile([P, 2 * H], U32, name="words1", align_bytes=64)
         x_codes = sb.tile([P, S], U32, name="x_codes", align_bytes=64)
@@ -100,32 +120,18 @@ def tile_picked_atzapolarpagew_none_p_kernel(
         bytes_by_t = plane1[:, S:].rearrange("p (l m t) -> p t l m", l=2, t=PACK)
         h = []
         for t in range(TILES):
-            dealt_words = sb.tile([P, 2, P], U32, name=f"dealt_words_{t}", tag="dealt_words", bufs=2, align_bytes=64)
+            dealt_words = sb.tile([P, 2, P], U32, name=f"dealt_words_{t}", tag=("even", "odd")[t % 2], align_bytes=64)
             dealt_bytes = sb.tile([P, 2, P], U8, name=f"dealt_bytes_{t}", align_bytes=64)
             nc.vector.tensor_copy(dealt_words[:], words_by_t[:, t])
             nc.vector.tensor_copy(dealt_bytes[:], bytes_by_t[:, t])
-            acc = psum.tile([P, S], F32, name=f"acc1_{t}")
-            for l in range(2):
-                nc.tensor.matmul_mx(
-                    out=acc[:],
-                    lhsT=dealt_words[:, l, :].bitcast(FP8X4),
-                    lhsT_scale=dealt_bytes[:, l, :],
-                    rhs=x_codes[:].bitcast(FP8X4),
-                    rhs_scale=plane1[:, :S],
-                    start=(l == 0),
-                    stop=(l == 1),
-                )
             h_t = sb.tile([P, S], F32, name=f"h_{t}")
-            if t == 0:
-                nc.scalar.activation(h_t[:], acc[:], ACT.Copy, scale=0.0625)
-            else:
-                nc.vector.tensor_scalar(h_t[:], acc[:], 0.0625, None, ALU.mult)
+            product(t, dealt_words, dealt_bytes, x_codes, plane1, h_t)
             h.append(h_t)
 
-        squares = sb.tile([P, TILES, W], F32, name="squares")
+        squares = sb.tile([P, TILES, W], F32, name="squares", tag="squares", align_bytes=64)
         rb = []
         for t in range(TILES):
-            pair = sb.tile([P, 2, W], F32, name=f"pair_{t}", tag=f"pair_{t}", align_bytes=64)
+            pair = sb.tile([P, 2, W], F32, name=f"pair_{t}")
             nc.scalar.activation(pair[:, 0, :], h[t][:].indirect(n1_sb[:]), ACT.Copy)
             nc.scalar.activation(pair[:, 1, :], h[t][:].indirect(n2_sb[:]), ACT.Copy)
             rb_t = sb.tile([P, W], F32, name=f"rb_{t}")
@@ -135,10 +141,10 @@ def tile_picked_atzapolarpagew_none_p_kernel(
             nc.vector.tensor_tensor(sq[:], pair[:], pair[:], ALU.mult)
             nc.vector.scalar_tensor_tensor(squares[:, t, :], sq[:, 0, :], 0.25, sq[:, 1, :], ALU.add, ALU.add)
 
-        bytes2 = sb.tile([P, 2 * H], U8, name="bytes2", tag=f"pair_{TILES - 1}", align_bytes=64)
+        bytes2 = sb.tile([P, 2 * H], U8, name="bytes2", tag=f"sq_{TILES - 1}", align_bytes=64)
         nc.vector.tensor_copy(bytes2[:, :H], d_scale_table[:].indirect(kc_sb[:]))
         nc.vector.tensor_copy(bytes2[:, H:], d_scale_table[:].indirect(kd_sb[:]))
-        place_scale_rows(nc.sync, plane2, bytes2)
+        place_scale_rows((nc.sync,), plane2, bytes2)
 
         def gather_half_of_codes(half, tag):
             codes = sb.tile([P, 2, HALF], U32, name=f"codes2_{half}", tag=tag, align_bytes=64)
@@ -147,14 +153,12 @@ def tile_picked_atzapolarpagew_none_p_kernel(
                 nc.vector.tensor_copy(codes[:, l, :], d_word_table[:].bitcast(U32).indirect(picks[:, columns]))
             return codes
 
-        codes2 = [gather_half_of_codes(0, f"sq_{TILES - 1}")]
-
         ub = [sb.tile([P, S], F32, name=f"ub_{t}") for t in range(TILES)]
         for t in range(TILES):
             nc.scalar.activation(ub[t][:].indirect(n2_sb[:]), rb[t][:], ACT.Copy)
         ra = sb.tile([P, TILES, W], F32, name="ra")
         nc.scalar.activation(ra[:], squares[:], ACT.Sqrt)
-        token_halves = [slice(0, S // 2), slice(S // 2, S)]
+        codes2 = [gather_half_of_codes(0, "squares")]
         z = sb.tile([P, S, PACK], BF16, name="z", tag="z", align_bytes=64)
         for t in range(TILES):
             nc.scalar.activation(ub[t][:].indirect(n1_sb[:]), ra[:, t, :], ACT.Copy)
@@ -170,26 +174,13 @@ def tile_picked_atzapolarpagew_none_p_kernel(
                 scales=z_plane[:, cols],
                 in_=z[:, cols, :].rearrange("p n t -> p (n t)"),
             )
-        codes2.append(gather_half_of_codes(1, "z"))
 
+        codes2.append(gather_half_of_codes(1, "z"))
+        plane2_by_list = plane2[:].rearrange("p (l m) -> p l m", l=2)
         for t in range(TILES):
-            acc = psum.tile([P, S], F32, name=f"acc2_{t}")
+            rows = slice(t * P, (t + 1) * P)
             half, first = divmod(t * P, HALF)
-            for cols in token_halves if t == 0 else [slice(0, S)]:
-                for l in range(2):
-                    nc.tensor.matmul_mx(
-                        out=acc[:, cols],
-                        lhsT=codes2[half][:, l, first : first + P].bitcast(FP8X4),
-                        lhsT_scale=plane2[:, l * H + t * P : l * H + (t + 1) * P],
-                        rhs=z_codes[:, cols].bitcast(FP8X4),
-                        rhs_scale=z_plane[:, cols],
-                        start=(l == 0),
-                        stop=(l == 1),
-                    )
-            if t == 0:
-                nc.scalar.activation(h2[t][:, :S], acc[:], ACT.Copy, scale=0.0625)
-            else:
-                nc.vector.tensor_scalar(h2[t][:, :S], acc[:], 0.0625, None, ALU.mult)
+            product(t, codes2[half][:, :, first : first + P], plane2_by_list[:, :, rows], z_codes, z_plane, h2[t])
 
         for t in range(TILES):
             at_n5 = sb.tile([P, S], F32, name=f"at_n5_{t}")

@@ -30,6 +30,7 @@ def tile_picked_atzapolarpagew_none_p_kernel(
     with ExitStack() as ctx:
         lists = ctx.enter_context(tc.tile_pool(name="lists", bufs=1))
         sb = ctx.enter_context(tc.tile_pool(name="sb", bufs=1))
+        reused = ctx.enter_context(tc.tile_pool(name="reused", bufs=1))
         psum = ctx.enter_context(tc.psum_pool(name="psum", bufs=1))
 
         def load_list(src, name):
@@ -104,26 +105,31 @@ def tile_picked_atzapolarpagew_none_p_kernel(
         for window in h2 + st:
             nc.vector.memset(window[:, S:], 0.0)
 
-        bytes1 = sb.tile([P, S + 2 * H], U8, name="bytes1", tag="odd", align_bytes=64)
+        bytes1 = reused.tile([P, S + 2 * H], U8, name="bytes1", align_bytes=64, offset=0)
         nc.vector.tensor_copy(bytes1[:, :S], x_scale_table[:].indirect(offs_sb[:]))
         nc.vector.tensor_copy(bytes1[:, S : S + H], d_scale_table[:].indirect(ka_sb[:]))
         nc.vector.tensor_copy(bytes1[:, S + H :], d_scale_table[:].indirect(kb_sb[:]))
         place_scale_rows((nc.scalar,), plane1, bytes1)
 
         words1 = sb.tile([P, 2 * H], U32, name="words1", align_bytes=64)
-        x_codes = sb.tile([P, S], U32, name="x_codes", align_bytes=64)
         nc.vector.tensor_copy(words1[:, :H], d_word_table[:].bitcast(U32).indirect(ka_sb[:]))
         nc.vector.tensor_copy(words1[:, H:], d_word_table[:].bitcast(U32).indirect(kb_sb[:]))
-        nc.vector.tensor_copy(x_codes[:], x_word_table[:].bitcast(U32).indirect(offs_sb[:]))
 
         words_by_t = words1[:].rearrange("p (l m t) -> p t l m", l=2, t=PACK)
         bytes_by_t = plane1[:, S:].rearrange("p (l m t) -> p t l m", l=2, t=PACK)
+        x_codes = reused.tile([P, S], U32, name="x_codes", align_bytes=64, offset=0)
         h = []
         for t in range(TILES):
-            dealt_words = sb.tile([P, 2, P], U32, name=f"dealt_words_{t}", tag=("even", "odd")[t % 2], align_bytes=64)
+            dealt_words = reused.tile(
+                [P, 2, P], U32, name=f"dealt_words_{t}", align_bytes=64, offset=1024 * (2 - t % 2)
+            )
             dealt_bytes = sb.tile([P, 2, P], U8, name=f"dealt_bytes_{t}", align_bytes=64)
             nc.vector.tensor_copy(dealt_words[:], words_by_t[:, t])
             nc.vector.tensor_copy(dealt_bytes[:], bytes_by_t[:, t])
+            if t == 0:
+                for cols in token_halves:
+                    picks = offs_sb[:, cols.start // 16 : cols.stop // 16]
+                    nc.vector.tensor_copy(x_codes[:, cols], x_word_table[:].bitcast(U32).indirect(picks))
             h_t = sb.tile([P, S], F32, name=f"h_{t}")
             product(t, dealt_words, dealt_bytes, x_codes, plane1, h_t)
             h.append(h_t)

from contextlib import ExitStack

import concourse.mybir as mybir

K, T, S, G, H, W, U = 512, 1024, 256, 2048, 512, 128, 512
FLOPS = 4 * 2 * K * H * S

F32 = mybir.dt.float32
BF16 = mybir.dt.bfloat16
I32 = mybir.dt.int32
U32 = mybir.dt.uint32
U16 = mybir.dt.uint16
U8 = mybir.dt.uint8
FP8X4 = mybir.dt.float8_e4m3fn_x4
ALU = mybir.AluOpType
ACT = mybir.ActivationFunctionType

P = 128
PACK = 4
TILES = H // P
BLOCKS = K // 32
SPARE = 16
HALF = H // 2


def tile_picked_atzapolarpagew_none_p_kernel(
    tc, x_words, x_scales, d_words, d_scales, gs, offs, ka, kb, n1, n2, kc, kd, n3, n4, n5, n6, out
):
    nc = tc.nc
    with ExitStack() as ctx:
        lists = ctx.enter_context(tc.tile_pool(name="lists", bufs=1))
        sb = ctx.enter_context(tc.tile_pool(name="sb", bufs=1))
        reused = ctx.enter_context(tc.tile_pool(name="reused", bufs=1))
        psum = ctx.enter_context(tc.psum_pool(name="psum", bufs=1))

        def load_list(src, name):
            tile = lists.tile(list(src.shape), U16, name=name)
            nc.sync.dma_start(tile[:], src)
            return tile

        def load_scale_rows(src, width, name):
            tile = sb.tile([P, width], U8, name=name, align_bytes=64)
            rows = src[0].bitcast(I32).unsqueeze(1).broadcast_to([BLOCKS, P // BLOCKS, width // 4])
            nc.sync.dma_start(tile[:].bitcast(I32), rows)
            return tile

        def load_words(src, width, name):
            tile = sb.tile([P, width], I32, name=name, align_bytes=64)
            nc.sync.dma_start(tile[:], src[0].rearrange("p n t -> p (n t)").bitcast(I32))
            return tile

        def place_scale_rows(queues, plane, gathered):
            for r in range(4):
                queues[r % len(queues)].dma_start(plane[:].bitcast(I32)[r:P:32, :], gathered[:].bitcast(I32)[8 * r : P : 32, :])

        token_halves = [slice(0, S // 2), slice(S // 2, S)]

        def product(t, words, scales, codes, plane, result):
            for cols in token_halves if t == 0 else [slice(0, S)]:
                acc = psum.tile([P, cols.stop - cols.start], F32, name="acc", bufs=8)
                for l in range(2):
                    nc.tensor.matmul_mx(
                        out=acc[:],
                        lhsT=words[:, l, :].bitcast(FP8X4),
                        lhsT_scale=scales[:, l, :],
                        rhs=codes[:, cols].bitcast(FP8X4),
                        rhs_scale=plane[:, cols],
                        start=(l == 0),
                        stop=(l == 1),
                    )
                if t == 0:
                    nc.scalar.activation(result[:, cols], acc[:], ACT.Copy, scale=0.0625)
                else:
                    nc.vector.tensor_scalar(result[:, cols], acc[:], 0.0625, None, ALU.mult)

        x_scale_table = load_scale_rows(x_scales, T, "x_scale_table")
        offs_sb = load_list(offs, "offs_sb")
        d_scale_table = load_scale_rows(d_scales, G, "d_scale_table")
        ka_sb = load_list(ka, "ka_sb")
        kb_sb = load_list(kb, "kb_sb")
        d_word_table = load_words(d_words, G, "d_word_table")
        x_word_table = load_words(x_words, T, "x_word_table")
        n1_sb = load_list(n1, "n1_sb")
        n2_sb = load_list(n2, "n2_sb")
        kc_sb = load_list(kc, "kc_sb")
        kd_sb = load_list(kd, "kd_sb")
        n5_sb = load_list(n5, "n5_sb")
        n6_sb = load_list(n6, "n6_sb")
        n3_sb = load_list(n3, "n3_sb")
        n4_sb = load_list(n4, "n4_sb")
        gs_sb = sb.tile([P, PACK], F32, name="gs_sb")
        nc.sync.dma_start(gs_sb[:], gs.rearrange("(p t) o -> p (t o)", t=PACK))

        one = sb.tile([P, 1], F32, name="one")
        unread = sb.tile([P, 1], F32, name="unread")
        nc.vector.memset(one[:], 1.0)
        nc.scalar.activation(unread[:], one[:], ACT.Sqrt)

        plane1 = sb.tile([P, S + 2 * H], U8, name="plane1", align_bytes=64)
        plane2 = sb.tile([P, 2 * H], U8, name="plane2", align_bytes=64)
        nc.vector.memset(plane1[:].bitcast(I32), 0)
        nc.vector.memset(plane2[:].bitcast(I32), 0)
        h2 = [sb.tile([P, S + SPARE], F32, name=f"h2_{t}") for t in range(TILES)]
        st = [sb.tile([P, S + SPARE], F32, name=f"st_{t}") for t in range(TILES)]
        for window in h2 + st:
            nc.vector.memset(window[:, S:], 0.0)

        bytes1 = reused.tile([P, S + 2 * H], U8, name="bytes1", align_bytes=64, offset=0)
        nc.vector.tensor_copy(bytes1[:, :S], x_scale_table[:].indirect(offs_sb[:]))
        nc.vector.tensor_copy(bytes1[:, S : S + H], d_scale_table[:].indirect(ka_sb[:]))
        nc.vector.tensor_copy(bytes1[:, S + H :], d_scale_table[:].indirect(kb_sb[:]))
        place_scale_rows((nc.scalar,), plane1, bytes1)

        words1 = sb.tile([P, 2 * H], U32, name="words1", align_bytes=64)
        nc.vector.tensor_copy(words1[:, :H], d_word_table[:].bitcast(U32).indirect(ka_sb[:]))
        nc.vector.tensor_copy(words1[:, H:], d_word_table[:].bitcast(U32).indirect(kb_sb[:]))

        words_by_t = words1[:].rearrange("p (l m t) -> p t l m", l=2, t=PACK)
        bytes_by_t = plane1[:, S:].rearrange("p (l m t) -> p t l m", l=2, t=PACK)
        x_codes = reused.tile([P, S], U32, name="x_codes", align_bytes=64, offset=0)
        h = []
        for t in range(TILES):
            dealt_words = reused.tile(
                [P, 2, P], U32, name=f"dealt_words_{t}", align_bytes=64, offset=1024 * (2 - t % 2)
            )
            dealt_bytes = sb.tile([P, 2, P], U8, name=f"dealt_bytes_{t}", align_bytes=64)
            nc.vector.tensor_copy(dealt_words[:], words_by_t[:, t])
            nc.vector.tensor_copy(dealt_bytes[:], bytes_by_t[:, t])
            if t == 0:
                for cols in token_halves:
                    picks = offs_sb[:, cols.start // 16 : cols.stop // 16]
                    nc.vector.tensor_copy(x_codes[:, cols], x_word_table[:].bitcast(U32).indirect(picks))
            h_t = sb.tile([P, S], F32, name=f"h_{t}")
            product(t, dealt_words, dealt_bytes, x_codes, plane1, h_t)
            h.append(h_t)

        squares = sb.tile([P, TILES, W], F32, name="squares", tag="squares", align_bytes=64)
        rb = []
        for t in range(TILES):
            pair = sb.tile([P, 2, W], F32, name=f"pair_{t}")
            nc.scalar.activation(pair[:, 0, :], h[t][:].indirect(n1_sb[:]), ACT.Copy)
            nc.scalar.activation(pair[:, 1, :], h[t][:].indirect(n2_sb[:]), ACT.Copy)
            rb_t = sb.tile([P, W], F32, name=f"rb_{t}")
            nc.vector.scalar_tensor_tensor(rb_t[:], pair[:, 0, :], -0.5, pair[:, 1, :], ALU.mult, ALU.add)
            rb.append(rb_t)
            sq = sb.tile([P, 2, W], F32, name=f"sq_{t}", tag=f"sq_{t}", align_bytes=64)
            nc.vector.tensor_tensor(sq[:], pair[:], pair[:], ALU.mult)
            nc.vector.scalar_tensor_tensor(squares[:, t, :], sq[:, 0, :], 0.25, sq[:, 1, :], ALU.add, ALU.add)

        bytes2 = sb.tile([P, 2 * H], U8, name="bytes2", tag=f"sq_{TILES - 1}", align_bytes=64)
        nc.vector.tensor_copy(bytes2[:, :H], d_scale_table[:].indirect(kc_sb[:]))
        nc.vector.tensor_copy(bytes2[:, H:], d_scale_table[:].indirect(kd_sb[:]))
        place_scale_rows((nc.sync,), plane2, bytes2)

        def gather_half_of_codes(half, tag):
            codes = sb.tile([P, 2, HALF], U32, name=f"codes2_{half}", tag=tag, align_bytes=64)
            columns = slice(half * HALF // 16, (half + 1) * HALF // 16)
            for l, picks in enumerate((kc_sb, kd_sb)):
                nc.vector.tensor_copy(codes[:, l, :], d_word_table[:].bitcast(U32).indirect(picks[:, columns]))
            return codes

        ub = [sb.tile([P, S], F32, name=f"ub_{t}") for t in range(TILES)]
        for t in range(TILES):
            nc.scalar.activation(ub[t][:].indirect(n2_sb[:]), rb[t][:], ACT.Copy)
        ra = sb.tile([P, TILES, W], F32, name="ra")
        nc.scalar.activation(ra[:], squares[:], ACT.Sqrt)
        codes2 = [gather_half_of_codes(0, "squares")]
        z = sb.tile([P, S, PACK], BF16, name="z", tag="z", align_bytes=64)
        for t in range(TILES):
            nc.scalar.activation(ub[t][:].indirect(n1_sb[:]), ra[:, t, :], ACT.Copy)
            pieces = token_halves if t == TILES - 1 else [slice(0, S)]
            for cols in pieces:
                nc.vector.tensor_scalar(z[:, cols, t], ub[t][:, cols], gs_sb[:, t : t + 1], None, ALU.mult)

        z_codes = sb.tile([P, S], U32, name="z_codes", align_bytes=64)
        z_plane = sb.tile([P, S], U8, name="z_plane", align_bytes=64)
        for cols in token_halves:
            nc.vector.quantize_mx(
                out=z_codes[:, cols].bitcast(FP8X4),
                scales=z_plane[:, cols],
                in_=z[:, cols, :].rearrange("p n t -> p (n t)"),
            )

        codes2.append(gather_half_of_codes(1, "z"))
        plane2_by_list = plane2[:].rearrange("p (l m) -> p l m", l=2)
        for t in range(TILES):
            rows = slice(t * P, (t + 1) * P)
            half, first = divmod(t * P, HALF)
            product(t, codes2[half][:, :, first : first + P], plane2_by_list[:, :, rows], z_codes, z_plane, h2[t])

        for t in range(TILES):
            at_n5 = sb.tile([P, S], F32, name=f"at_n5_{t}")
            nc.scalar.activation(at_n5[:], h2[t][:].indirect(n5_sb[:]), ACT.Copy)
            nc.vector.tensor_tensor(st[t][:, :S], h2[t][:, :S], at_n5[:], ALU.subtract)
        up = []
        for t in range(TILES):
            at_n6 = sb.tile([P, S], F32, name=f"at_n6_{t}")
            nc.scalar.activation(at_n6[:], st[t][:].indirect(n6_sb[:]), ACT.Copy)
            up_t = sb.tile([P, S], F32, name=f"up_{t}")
            nc.vector.tensor_tensor(up_t[:], st[t][:, :S], at_n6[:], ALU.max)
            up.append(up_t)
        page = [sb.tile([P, U], F32, name=f"page_{t}") for t in range(TILES)]
        for t in range(TILES):
            nc.scalar.activation(page[t][:].indirect(n3_sb[:]), st[t][:, :S], ACT.Copy)
        for t in range(TILES):
            nc.scalar.activation(page[t][:].indirect(n4_sb[:]), up[t][:], ACT.Copy)
            nc.sync.dma_start(out[t * P : (t + 1) * P, :], page[t][:])
